import numpy as np
import ml_dtypes


def mxq(x, axis, fmt="e4m3"):
    dtype, down = {"e4m3": (ml_dtypes.float8_e4m3fn, 7), "e5m2": (ml_dtypes.float8_e5m2, 14)}[fmt]
    v = np.moveaxis(np.asarray(x, np.float32).astype(ml_dtypes.bfloat16).astype(np.float64), axis, -1)
    blocks = v.reshape(v.shape[:-1] + (-1, 32))
    amax = np.abs(blocks).max(-1, keepdims=True)
    byte = np.maximum(np.where(amax > 0, np.frexp(amax)[1] - 1 + 127, 0) - down, 1)
    scale = np.exp2(byte - 127.0)
    codes = (blocks / scale).astype(np.float32).astype(dtype).astype(np.float64)
    return np.moveaxis((codes * scale).reshape(v.shape), -1, axis)


WIDE = False


def mx_kscale(k):
    if not WIDE:
        return np.ones(k)
    levels = np.array([10, -10, 5, -5, 0])
    if k % 512:
        return np.exp2(np.random.permutation(np.resize(levels, k // 32))).repeat(32)
    a = np.empty((k // 512, 16))
    for p in range(k // 512):
        a[p, :8] = np.random.permutation(np.resize(levels, 8))
        for g in range(8):
            far = levels[np.abs(levels - a[p, g]) >= 10]
            a[p, g + 8] = far[np.random.randint(len(far))]
    return np.exp2(a.ravel()).repeat(32)


def f64(x):
    return np.asarray(x).astype(np.float64)


def striped(idx):
    return np.tile(idx.reshape(-1, 16).T, (8, 1)).astype(np.uint16)


def unstriped(offs):
    return offs[:16].T.reshape(-1).astype(np.int64)


E2M1 = np.array([0.0, 0.5, 1.0, 1.5, 2.0, 3.0, 4.0, 6.0, -0.0, -0.5, -1.0, -1.5, -2.0, -3.0, -4.0, -6.0])


def pack_weight(w, fmt):
    k, n = w.shape
    w = f64(np.asarray(w, np.float32).astype(ml_dtypes.bfloat16)).reshape(k // 32, 32, n)
    amax = np.abs(w).max(1)
    if fmt == "e4m3":
        byte = np.frexp(amax)[1] - 1 + 127 - 7
    else:
        mant, ex = np.frexp(amax / 6.0)
        byte = np.where(mant > 0.5, ex, ex - 1) + 127
    byte = np.clip(np.where(amax > 0, byte, 1), 1, 254)
    scaled = (w * np.exp2(127.0 - byte)[:, None, :]).reshape(k, n).astype(np.float32)
    by_word = np.ascontiguousarray(scaled.reshape(k // 512, 128, 4, n).transpose(0, 1, 3, 2))
    if fmt == "e4m3":
        words = by_word.astype(ml_dtypes.float8_e4m3fn).view(np.uint8)
    else:
        c = by_word.astype(ml_dtypes.float4_e2m1fn).view(np.uint8) & 0xF
        words = (c[..., 0::2] | (c[..., 1::2] << 4)).reshape(k // 512, 128, 2 * n)
    return np.ascontiguousarray(words), np.ascontiguousarray(byte.astype(np.uint8).reshape(k // 512, 16, n))


def unpack_weight(words, scales, fmt):
    g, _, n = scales.shape
    words = np.ascontiguousarray(words).reshape(g, 128, n, -1)
    if fmt == "e4m3":
        vals = words.view(ml_dtypes.float8_e4m3fn).astype(np.float64)
    else:
        nib = np.empty((g, 128, n, 4), np.uint8)
        nib[..., 0::2] = words & 0xF
        nib[..., 1::2] = words >> 4
        vals = E2M1[nib]
    vals = vals * np.repeat(np.exp2(scales.astype(np.float64) - 127.0), 8, axis=1)[..., None]
    return vals.transpose(0, 1, 3, 2).reshape(g * 512, n)


def gelu(v):
    return 0.5 * v * (1.0 + np.tanh(np.sqrt(2.0 / np.pi) * (v + 0.044715 * v**3)))


def bf(x):
    return np.asarray(x, np.float32).astype(ml_dtypes.bfloat16)


def planes(Y):
    n, m = Y.shape
    b = f64(bf(Y)).reshape(n // 32, 32, m)
    amax = np.abs(b).max(1)
    byte = np.clip(np.where(amax > 0, np.frexp(amax)[1] - 1 + 127 - 7, 1), 1, 254)
    codes = (b * np.exp2(127.0 - byte)[:, None, :]).reshape(n, m).astype(np.float32).astype(ml_dtypes.float8_e4m3fn).view(np.uint8)
    words = codes.reshape(n // 512, 128, 4, m).transpose(0, 1, 3, 2)
    return np.ascontiguousarray(words), np.ascontiguousarray(byte.astype(np.uint8).reshape(n // 512, 16, m))


K, T, S, H, T2, P, N = 512, 4096, 1024, 1024, 2048, 1024, 384


def setup_inputs():
    n = np.random.standard_normal
    s = mx_kscale(K)[:, None]
    u = mx_kscale(H)[:, None]
    d = {}
    d["tab_words"], d["tab_scales"] = pack_weight(n((K, T)) * s, "e4m3")
    d["offs"] = striped(np.random.permutation(T)[:S])
    d["offs2"] = striped(np.random.permutation(T2)[:S])
    d["offs3"] = striped(np.random.permutation(T2)[:P])
    d["w1"] = (1.3 * n((K, H)) / s * u.T / K ** 0.5).astype(np.float32)
    d["w2"] = (1.3 * n((K, H)) / s / K ** 0.5).astype(np.float32)
    d["w3_words"], d["w3_scales"] = pack_weight(1.5 * n((K, H)) / s / K ** 0.5, "e4m3")
    d["page0"] = (n((H, T2)) * u).astype(np.float32)
    d["wgs"] = np.exp(0.3 * n((128, S))).astype(np.float32)
    d["bh"] = (0.8 * n(H) * u[:, 0]).astype(np.float32)
    d["w4_words"], d["w4_scales"] = pack_weight(n((H, N)) / u / H ** 0.5, "e2m1")
    return d


def reference(tab_words, tab_scales, offs, offs2, offs3, w1, w2, w3_words, w3_scales, page0, wgs, bh, w4_words, w4_scales):
    v = unpack_weight(tab_words, tab_scales, "e4m3")[:, unstriped(offs)]
    a1 = mxq(f64(w1), 0, "e4m3").T @ v
    a2 = mxq(f64(w2), 0, "e4m3").T @ v
    a3 = unpack_weight(w3_words, w3_scales, "e4m3").T @ v
    h = a1 * a2 / (1.0 + np.abs(a3))
    page = f64(page0).copy()
    page[:, unstriped(offs2)] = np.tile(f64(wgs), (H // 128, 1)) * h
    x = page[:, unstriped(offs3)] + f64(bh)[:, None]
    y = unpack_weight(w4_words, w4_scales, "e2m1").T @ mxq(x, 0, "e4m3")
    words, scales = planes(page)
    return y, page, words, scales

@@ -1,0 +1,350 @@
+from contextlib import ExitStack
+
+import concourse.mybir as mybir
+
+K, T, S, H, T2, NP, N = 512, 4096, 1024, 1024, 2048, 1024, 384
+FLOPS = 2 * K * H * S * 3 + 2 * H * N * NP
+
+F32 = mybir.dt.float32
+BF16 = mybir.dt.bfloat16
+I32 = mybir.dt.int32
+U32 = mybir.dt.uint32
+U16 = mybir.dt.uint16
+U8 = mybir.dt.uint8
+FP8X4 = mybir.dt.float8_e4m3fn_x4
+FP4X4 = mybir.dt.float4_e2m1fn_x4
+ACT = mybir.ActivationFunctionType
+ALU = mybir.AluOpType
+
+P = 128
+PACK = 4
+GROUP = P * PACK
+BANK = 512
+GROUPS = H // GROUP
+SLICES = GROUPS * PACK
+CHUNKS = T2 // BANK
+
+
+def tile_list_digester_feed_features_kernel(
+    tc, tab_words, tab_scales, offs, offs2, offs3, w1, w2, w3_words, w3_scales, page0, wgs, bh, w4_words, w4_scales,
+    out_0, out_1, out_2, out_3,
+):
+    nc = tc.nc
+    with ExitStack() as ctx:
+        lists = ctx.enter_context(tc.tile_pool(name="lists", bufs=1))
+        keep = ctx.enter_context(tc.tile_pool(name="keep", bufs=1))
+        work = ctx.enter_context(tc.tile_pool(name="work", bufs=1))
+        psum = ctx.enter_context(tc.psum_pool(name="psum", bufs=1))
+
+        def load_scale_rows(queue, plane, rows):
+            for q in range(4):
+                queue.dma_start(out=plane[32 * q : 32 * q + 4].bitcast(I32), in_=rows[4 * q : 4 * q + 4].bitcast(I32))
+
+        idx = lists.tile([P, S // 16], U16, name="idx")
+        idx2 = lists.tile([P, S // 16], U16, name="idx2")
+        idx3 = lists.tile([P, NP // 16], U16, name="idx3")
+
+        tab_w = keep.tile([P, T], U32, name="tab_w", tag="table", align_bytes=64)
+        tab_s = keep.tile([P, T], U8, name="tab_s", align_bytes=64)
+        w3_raw_w = [keep.tile([P, GROUP], I32, name=f"w3_raw_w{g}", align_bytes=64) for g in range(GROUPS)]
+        w3_raw_s = keep.tile([P, H], U8, name="w3_raw_s", align_bytes=64)
+        w4_w = keep.tile([P, GROUPS, 2 * N], U8, name="w4_w", align_bytes=64)
+        w4_s = keep.tile([P, GROUPS, N], U8, name="w4_s", align_bytes=64)
+        bias = keep.tile([P, GROUPS, PACK], F32, name="bias")
+        gain_first = keep.tile([P, 1, S], F32, name="gain_first")
+        gains = [gain_first[:, 0, :]]
+        pages = [keep.tile([P, T2], F32, name=f"page{i}") for i in range(SLICES)]
+        warm = keep.tile([P, 2], F32, name="warm")
+
+        nc.vector.memset(tab_s[:].bitcast(I32), 0)
+        nc.gpsimd.memset(w3_raw_s[:].bitcast(I32), 0)
+        nc.vector.memset(w4_s[:].rearrange("p g n -> p (g n)").bitcast(I32), 0)
+        nc.vector.memset(warm[:], 1.0)
+
+        def slot(name, tag, shape, dtype):
+            return work.tile(shape, dtype, name=name, tag=tag, align_bytes=64)
+
+        def quad_tile(name, c):
+            return slot(name, f"quad{c}", [P, PACK, BANK], F32)
+
+        def load_weight(w, g, name, c):
+            raw = quad_tile(name, c)
+            nc.sync.dma_start(out=raw[:], in_=w[:, g * GROUP : (g + 1) * GROUP].rearrange("(p i) c -> p i c", i=PACK))
+            return raw
+
+        def load_gains(tile, first, count):
+            rows = wgs.rearrange("(q t) j -> q t j", t=PACK)[:, first : first + count, :]
+            for a in range(4):
+                nc.sync.dma_start(out=tile[32 * a : 32 * a + 32], in_=rows)
+
+        page_in = page0.rearrange("(g p t) m -> g t p m", p=P, t=PACK)
+        page_out = out_1.rearrange("(g p t) m -> g t p m", p=P, t=PACK)
+
+        def load_w3_words(g):
+            words = w3_words[0].rearrange("p c i -> p (c i)").bitcast(I32)
+            nc.sync.dma_start(out=w3_raw_w[g][:], in_=words[:, g * GROUP : (g + 1) * GROUP])
+
+        def load_page(i):
+            nc.sync.dma_start(out=pages[i][:], in_=page_in[i // PACK, i % PACK])
+
+        nc.sync.dma_start(idx[:], offs)
+        nc.sync.dma_start(out=tab_w[:].bitcast(I32), in_=tab_words[0].rearrange("p t i -> p (t i)").bitcast(I32))
+        load_scale_rows(nc.sync, tab_s, tab_scales[0])
+        load_scale_rows(nc.gpsimd, w3_raw_s, w3_scales[0])
+        nc.scalar.activation(warm[:, 1:2], warm[:, 0:1], ACT.Abs_reciprocal_sqrt)
+        load_w3_words(0)
+        raw = {}
+        raw[0, 0] = load_weight(w1, 0, "w1_raw0", 0)
+        raw[1, 0] = load_weight(w2, 0, "w2_raw0", 1)
+        load_gains(gain_first, 0, 1)
+        nc.sync.dma_start(idx2[:], offs2)
+        load_page(0)
+
+        def load_rest():
+            gain_rest = keep.tile([P, PACK - 1, S], F32, name="gain_rest", tag="table", align_bytes=64)
+            gains.extend(gain_rest[:, t, :] for t in range(PACK - 1))
+            load_gains(gain_rest, 1, PACK - 1)
+            load_page(1)
+            nc.sync.dma_start(idx3[:], offs3)
+            load_w3_words(1)
+            raw[0, 1] = load_weight(w1, 1, "w1_raw1", 2)
+            load_page(2)
+            raw[1, 1] = load_weight(w2, 1, "w2_raw1", 3)
+            for i in range(PACK - 1, SLICES):
+                load_page(i)
+            nc.sync.dma_start(out=bias[:], in_=bh.rearrange("(g p t) -> p g t", p=P, t=PACK))
+            nc.sync.dma_start(out=w4_w[:].bitcast(I32), in_=w4_words.rearrange("g p c -> p g c").bitcast(I32))
+            load_scale_rows(nc.sync, w4_s, w4_scales.rearrange("g q n -> q g n"))
+
+        v_w = [keep.tile([P, BANK], U32, name=f"v_w{h}", align_bytes=64) for h in range(2)]
+        v_s = [keep.tile([P, BANK], U8, name=f"v_s{h}", align_bytes=64) for h in range(2)]
+
+        def gather_table(h):
+            part = idx[:, h * 32 : (h + 1) * 32]
+            nc.vector.tensor_copy(v_w[h][:], tab_w[:].indirect(part))
+            nc.vector.tensor_copy(v_s[h][:], tab_s[:].indirect(part))
+
+        codes = [[keep.tile([P, GROUP], I32, name=f"w{n}_codes{g}", align_bytes=64) for g in range(GROUPS)] for n in range(3)]
+        scales = [[keep.tile([P, GROUP], U8, name=f"w{n}_scales{g}", align_bytes=64) for g in range(GROUPS)] for n in range(3)]
+
+        def deal_w3(g):
+            cols = slice(g * GROUP, (g + 1) * GROUP)
+            for dst, src in ((codes[2][g], w3_raw_w[g][:]), (scales[2][g], w3_raw_s[:, cols])):
+                nc.vector.tensor_copy(
+                    out=dst[:].rearrange("p (t m) -> p t m", t=PACK), in_=src.rearrange("p (m t) -> p t m", t=PACK)
+                )
+
+        def woven_tile(name, tag):
+            return slot(name, tag, [P, BANK * PACK], BF16)
+
+        def round_weight(n, g, engine):
+            woven = woven_tile(f"w{n}_woven{g}", f"woven{n}")
+            dst = woven[:].rearrange("p (t m i) -> p m i t", t=PACK, i=PACK)
+            src = raw[n, g][:].rearrange("p i (m t) -> p m i t", t=PACK)
+            if engine == "scalar":
+                nc.scalar.copy(out=dst, in_=src)
+            else:
+                nc.vector.tensor_copy(out=dst, in_=src)
+            return woven
+
+        def quantize_weight(n, g, woven):
+            nc.vector.quantize_mx(out=codes[n][g][:].bitcast(FP8X4), scales=scales[n][g][:], in_=woven[:])
+
+        def product(n, i, h, tag, bufs):
+            g, t = divmod(i, PACK)
+            cols = slice(t * P, (t + 1) * P)
+            acc = psum.tile([P, BANK], F32, name=f"a{n}_{i}_{h}", tag=tag, bufs=bufs)
+            nc.tensor.matmul_mx(
+                out=acc[:], lhsT=codes[n][g][:, cols].bitcast(FP8X4), lhsT_scale=scales[n][g][:, cols],
+                rhs=v_w[h][:].bitcast(FP8X4), rhs_scale=v_s[h][:], start=True, stop=True,
+            )
+            return acc
+
+        damp, value, other = {}, {}, {}
+        on_gpsimd = (2, 3, 4, 5, 6, 7)
+        halves = [slice(h * BANK, (h + 1) * BANK) for h in range(2)]
+
+        def stage_damp(i, parts):
+            damp[i] = slot(f"damp{i}", f"damp{i % 3}", [P, S], F32)
+            for part in parts:
+                for h in range(part.start // BANK, part.stop // BANK):
+                    a3 = product(2, i, h, "a3", 2)
+                    nc.scalar.activation(damp[i][:, halves[h]], a3[:], ACT.Abs)
+                nc.scalar.activation(damp[i][:, part], damp[i][:, part], ACT.Abs_reciprocal_sqrt, bias=1.0)
+                nc.scalar.activation(damp[i][:, part], damp[i][:, part], ACT.Square)
+
+        def stage_value(i):
+            value[i] = slot(f"value{i}", f"value{i % 3}", [P, S], F32)
+            for h in range(2):
+                a2 = product(1, i, h, "a2", 2)
+                nc.scalar.copy(out=value[i][:, halves[h]], in_=a2[:])
+            if i in on_gpsimd:
+                other[i] = slot(f"other{i}", f"other{i % 2}", [P, S], F32)
+                for h in range(2):
+                    a1 = product(0, i, h, "a1", 4)
+                    nc.scalar.copy(out=other[i][:, halves[h]], in_=a1[:])
+
+        def stage_multiply(i):
+            nc.gpsimd.tensor_tensor(damp[i][:], damp[i][:], gains[i % PACK], ALU.mult)
+            if i in on_gpsimd:
+                nc.gpsimd.tensor_tensor(value[i][:], value[i][:], other[i][:], ALU.mult)
+            nc.gpsimd.tensor_tensor(value[i][:], value[i][:], damp[i][:], ALU.mult)
+
+        quads = {}
+
+        def store_page(i):
+            nc.sync.dma_start(out=page_out[i // PACK, i % PACK], in_=pages[i][:])
+
+        def stage_scatter(i):
+            if i not in on_gpsimd:
+                for h in range(2):
+                    a1 = product(0, i, h, "a1", 4)
+                    nc.vector.tensor_tensor(value[i][:, halves[h]], a1[:], value[i][:, halves[h]], ALU.mult)
+            nc.vector.tensor_copy(pages[i][:].indirect(idx2[:]), value[i][:])
+
+        def first_slice():
+            stage_damp(0, halves)
+            value[0] = slot("value0", "value0", [P, S], F32)
+            for h in range(2):
+                nc.gpsimd.tensor_tensor(damp[0][:, halves[h]], damp[0][:, halves[h]], gains[0][:, halves[h]], ALU.mult)
+            for h in range(2):
+                a2 = product(1, 0, h, "a2", 2)
+                nc.vector.tensor_tensor(value[0][:, halves[h]], a2[:], damp[0][:, halves[h]], ALU.mult)
+
+        def regroup(i):
+            g, t = divmod(i, PACK)
+            if t == 0:
+                quads[g] = [quad_tile(f"quad{g}_{c}", c) for c in range(CHUNKS)]
+            for c in range(CHUNKS):
+                nc.sync.dma_start(out=quads[g][c][:, t, :], in_=pages[i][:, c * BANK : (c + 1) * BANK])
+
+        page_woven, page_scales = {}, {}
+
+        def weave(engine, dst, src):
+            dst = dst.rearrange("p (c i t) -> p c t i", i=4, t=PACK)
+            src = src.rearrange("p t (c i) -> p c t i", i=4)
+            if engine == "scalar":
+                nc.scalar.copy(out=dst, in_=src)
+            elif engine == "vector":
+                nc.vector.tensor_copy(out=dst, in_=src)
+            else:
+                nc.gpsimd.tensor_scalar(dst, src, 1.0, 0.0, ALU.mult, ALU.add)
+
+        def round_page(g, c, tag, engine):
+            page_woven[g, c] = woven_tile(f"page_woven{g}_{c}", tag)
+            weave(engine, page_woven[g, c][:], quads[g][c][:])
+
+        def quantize_page(g, c):
+            if c == 0:
+                page_scales[g] = work.tile([P, T2], U8, name=f"page_scales{g}", tag="page_scales", bufs=2, align_bytes=64)
+            cols = slice(c * BANK, (c + 1) * BANK)
+            words = work.tile([P, BANK], I32, name=f"page_words{g}_{c}", tag="page_words", bufs=3, align_bytes=64)
+            nc.vector.quantize_mx(out=words[:].bitcast(FP8X4), scales=page_scales[g][:, cols], in_=page_woven[g, c][:])
+            nc.sync.dma_start(out=out_2[g].rearrange("p m t -> p (m t)").bitcast(I32)[:, cols], in_=words[:])
+            if c == CHUNKS - 1:
+                for q in range(4):
+                    nc.sync.dma_start(
+                        out=out_3[g, 4 * q : 4 * q + 4].bitcast(I32), in_=page_scales[g][32 * q : 32 * q + 4].bitcast(I32)
+                    )
+
+        x_rows, x_woven = {}, {}
+        x_codes = [[keep.tile([P, BANK], I32, name=f"x_codes{g}_{h}", align_bytes=64) for h in range(2)] for g in range(GROUPS)]
+        x_scales = [[keep.tile([P, BANK], U8, name=f"x_scales{g}_{h}", align_bytes=64) for h in range(2)] for g in range(GROUPS)]
+
+        picked = [keep.tile([P, NP], F32, name=f"picked{t}") for t in range(PACK)]
+
+        def gather_page(i, cols):
+            part = idx3[:, cols.start // 16 : cols.stop // 16]
+            nc.vector.tensor_copy(picked[i % PACK][:, cols], pages[i][:].indirect(part))
+
+        def add_bias(i, cols):
+            g, t = divmod(i, PACK)
+            if g not in x_rows:
+                x_rows[g] = slot(f"x_rows{g}", f"damp{2 - g}", [P, PACK, NP], BF16)
+            nc.gpsimd.tensor_scalar(x_rows[g][:, t, cols], picked[t][:, cols], 1.0, bias[:, g, t : t + 1], ALU.mult, ALU.add)
+
+        def weave_x(g, h, tag, engine):
+            x_woven[g, h] = woven_tile(f"x_woven{g}_{h}", tag)
+            weave(engine, x_woven[g, h][:], x_rows[g][:, :, halves[h]])
+
+        def quantize_x(g, h):
+            nc.vector.quantize_mx(out=x_codes[g][h][:].bitcast(FP8X4), scales=x_scales[g][h][:], in_=x_woven[g, h][:])
+
+        def features(h):
+            for n in range(N // P):
+                tag, bufs = (("a1", 4), ("a2", 2), ("a3", 2))[n]
+                acc = psum.tile([P, BANK], F32, name=f"y{n}_{h}", tag=tag, bufs=bufs)
+                for g in range(GROUPS):
+                    nc.tensor.matmul_mx(
+                        out=acc[:], lhsT=w4_w[:, g, 2 * n * P : 2 * (n + 1) * P].bitcast(FP4X4),
+                        lhsT_scale=w4_s[:, g, n * P : (n + 1) * P],
+                        rhs=x_codes[g][h][:].bitcast(FP8X4), rhs_scale=x_scales[g][h][:],
+                        start=(g == 0), stop=(g == GROUPS - 1),
+                    )
+                staged = slot(f"y_staged{n}_{h}", (f"value{n}" if h == 0 else ("other0", "other1", "damp0")[n]), [P, BANK], F32)
+                if True:
+                    nc.scalar.copy(out=staged[:], in_=acc[:])
+                else:
+                    nc.vector.tensor_copy(out=staged[:], in_=acc[:])
+                nc.sync.dma_start(out=out_0[n * P : (n + 1) * P, h * BANK : (h + 1) * BANK], in_=staged[:])
+
+        whole = [slice(0, S)]
+        gather_table(0)
+        deal_w3(0)
+        woven1 = round_weight(0, 0, "scalar")
+        gather_table(1)
+        load_rest()
+        woven2 = round_weight(1, 0, "vector")
+        quantize_weight(1, 0, woven2)
+        quantize_weight(0, 0, woven1)
+        first_slice()
+        for i in range(1, 3):
+            stage_damp(i, whole)
+            stage_value(i)
+            stage_multiply(i)
+        last = SLICES - 1
+        for i in range(last):
+            stage_scatter(i)
+            if i == 0:
+                deal_w3(1)
+                woven1 = round_weight(0, 1, "scalar")
+                woven2 = round_weight(1, 1, "scalar")
+                quantize_weight(0, 1, woven1)
+                quantize_weight(1, 1, woven2)
+            if i + 3 < SLICES:
+                stage_damp(i + 3, whole)
+                stage_value(i + 3)
+                stage_multiply(i + 3)
+            if i == PACK:
+                for k in range(PACK):
+                    add_bias(k, whole[0])
+                for c in range(CHUNKS):
+                    round_page(0, c, f"woven{c % 3}", "scalar")
+                    quantize_page(0, c)
+                for h in range(2):
+                    weave_x(0, h, f"woven{1 + h}", "scalar")
+                    quantize_x(0, h)
+            gather_page(i, whole[0])
+            if i >= PACK:
+                add_bias(i, whole[0])
+            regroup(i)
+            store_page(i)
+        stage_scatter(last)
+        regroup(last)
+        store_page(last)
+        for h in range(2):
+            gather_page(last, halves[h])
+            add_bias(last, halves[h])
+            weave_x(1, h, f"woven{h}", "scalar")
+        round_page(1, 3, "value2", "gpsimd")
+        round_page(1, 0, "woven2", "vector")
+        round_page(1, 1, "value0", "vector")
+        quantize_x(1, 0)
+        quantize_page(1, 0)
+        quantize_page(1, 1)
+        quantize_x(1, 1)
+        round_page(1, 2, "value1", "vector")
+        quantize_page(1, 2)
+        quantize_page(1, 3)
+        for h in range(2):
+            features(h)

@@ -20,9 +20,16 @@ P = 128
 PACK = 4
 GROUP = P * PACK
 BANK = 512
+PSUM_BANKS = 8
+QUADRANT = 32
+QUADRANT_ORDER = (0, 2, 1, 3)
+LIST_ROWS = 16
+RUN = 4
 GROUPS = H // GROUP
 SLICES = GROUPS * PACK
+LAST = SLICES - 1
 CHUNKS = T2 // BANK
+AHEAD = 3
 
 
 def tile_list_digester_feed_features_kernel(
@@ -36,180 +43,167 @@ def tile_list_digester_feed_features_kernel(
         work = ctx.enter_context(tc.tile_pool(name="work", bufs=1))
         psum = ctx.enter_context(tc.psum_pool(name="psum", bufs=1))
 
-        def load_scale_rows(queue, plane, rows):
-            for q in range(4):
-                queue.dma_start(out=plane[32 * q : 32 * q + 4].bitcast(I32), in_=rows[4 * q : 4 * q + 4].bitcast(I32))
+        def lodge(name, room, shape, dtype):
+            return work.tile(shape, dtype, name=name, tag=room, align_bytes=64)
 
-        idx = lists.tile([P, S // 16], U16, name="idx")
-        idx2 = lists.tile([P, S // 16], U16, name="idx2")
-        idx3 = lists.tile([P, NP // 16], U16, name="idx3")
+        def bank(name):
+            return psum.tile([P, BANK], F32, name=name, tag="bank", bufs=PSUM_BANKS)
 
-        tab_w = keep.tile([P, T], U32, name="tab_w", tag="table", align_bytes=64)
-        tab_s = keep.tile([P, T], U8, name="tab_s", align_bytes=64)
-        w3_raw_w = [keep.tile([P, GROUP], I32, name=f"w3_raw_w{g}", align_bytes=64) for g in range(GROUPS)]
+        halves = [slice(h * BANK, (h + 1) * BANK) for h in range(2)]
+        whole = slice(0, NP)
+
+        idx = lists.tile([P, S // LIST_ROWS], U16, name="idx")
+        idx2 = lists.tile([P, S // LIST_ROWS], U16, name="idx2")
+        idx3 = lists.tile([P, NP // LIST_ROWS], U16, name="idx3")
+
+        def entries(offsets, cols):
+            return offsets[:, cols.start // LIST_ROWS : cols.stop // LIST_ROWS]
+
+        tab_w = lodge("tab_w", "table", [P, T], U32)
+        tab_s = lodge("tab_s", "woven2", [P, T], U8)
+        w3_raw_w = keep.tile([P, H], I32, name="w3_raw_w", align_bytes=64)
         w3_raw_s = keep.tile([P, H], U8, name="w3_raw_s", align_bytes=64)
         w4_w = keep.tile([P, GROUPS, 2 * N], U8, name="w4_w", align_bytes=64)
         w4_s = keep.tile([P, GROUPS, N], U8, name="w4_s", align_bytes=64)
         bias = keep.tile([P, GROUPS, PACK], F32, name="bias")
-        gain_first = keep.tile([P, 1, S], F32, name="gain_first")
-        gains = [gain_first[:, 0, :]]
+        gains = [keep.tile([P, S], F32, name=f"gain{t}") for t in range(PACK)]
         pages = [keep.tile([P, T2], F32, name=f"page{i}") for i in range(SLICES)]
-        warm = keep.tile([P, 2], F32, name="warm")
 
         nc.vector.memset(tab_s[:].bitcast(I32), 0)
-        nc.gpsimd.memset(w3_raw_s[:].bitcast(I32), 0)
+        nc.vector.memset(w3_raw_s[:].bitcast(I32), 0)
         nc.vector.memset(w4_s[:].rearrange("p g n -> p (g n)").bitcast(I32), 0)
-        nc.vector.memset(warm[:], 1.0)
 
-        def slot(name, tag, shape, dtype):
-            return work.tile(shape, dtype, name=name, tag=tag, align_bytes=64)
+        def load_scale_rows(plane, rows):
+            for q in QUADRANT_ORDER:
+                nc.sync.dma_start(
+                    out=plane[QUADRANT * q : QUADRANT * q + 4].bitcast(I32), in_=rows[4 * q : 4 * q + 4].bitcast(I32)
+                )
 
         def quad_tile(name, c):
-            return slot(name, f"quad{c}", [P, PACK, BANK], F32)
+            return lodge(name, f"quad{c}", [P, PACK, BANK], F32)
 
-        def load_weight(w, g, name, c):
-            raw = quad_tile(name, c)
-            nc.sync.dma_start(out=raw[:], in_=w[:, g * GROUP : (g + 1) * GROUP].rearrange("(p i) c -> p i c", i=PACK))
-            return raw
+        raw = {}
 
-        def load_gains(tile, first, count):
-            rows = wgs.rearrange("(q t) j -> q t j", t=PACK)[:, first : first + count, :]
-            for a in range(4):
-                nc.sync.dma_start(out=tile[32 * a : 32 * a + 32], in_=rows)
+        def load_weight(n, g):
+            raw[n, g] = quad_tile(f"w{n + 1}_raw{g}", 2 * g + n)
+            cols = (w1, w2)[n][:, g * GROUP : (g + 1) * GROUP]
+            nc.sync.dma_start(out=raw[n, g][:], in_=cols.rearrange("(p i) c -> p i c", i=PACK))
+
+        def load_gain(t):
+            rows = wgs.rearrange("(q t) j -> t q j", t=PACK)[t]
+            for q in QUADRANT_ORDER:
+                nc.sync.dma_start(out=gains[t][QUADRANT * q : QUADRANT * (q + 1)], in_=rows)
 
         page_in = page0.rearrange("(g p t) m -> g t p m", p=P, t=PACK)
         page_out = out_1.rearrange("(g p t) m -> g t p m", p=P, t=PACK)
 
-        def load_w3_words(g):
-            words = w3_words[0].rearrange("p c i -> p (c i)").bitcast(I32)
-            nc.sync.dma_start(out=w3_raw_w[g][:], in_=words[:, g * GROUP : (g + 1) * GROUP])
-
         def load_page(i):
             nc.sync.dma_start(out=pages[i][:], in_=page_in[i // PACK, i % PACK])
-
-        nc.sync.dma_start(idx[:], offs)
-        nc.sync.dma_start(out=tab_w[:].bitcast(I32), in_=tab_words[0].rearrange("p t i -> p (t i)").bitcast(I32))
-        load_scale_rows(nc.sync, tab_s, tab_scales[0])
-        load_scale_rows(nc.gpsimd, w3_raw_s, w3_scales[0])
-        nc.scalar.activation(warm[:, 1:2], warm[:, 0:1], ACT.Abs_reciprocal_sqrt)
-        load_w3_words(0)
-        raw = {}
-        raw[0, 0] = load_weight(w1, 0, "w1_raw0", 0)
-        raw[1, 0] = load_weight(w2, 0, "w2_raw0", 1)
-        load_gains(gain_first, 0, 1)
-        nc.sync.dma_start(idx2[:], offs2)
-        load_page(0)
-
-        def load_rest():
-            gain_rest = keep.tile([P, PACK - 1, S], F32, name="gain_rest", tag="table", align_bytes=64)
-            gains.extend(gain_rest[:, t, :] for t in range(PACK - 1))
-            load_gains(gain_rest, 1, PACK - 1)
-            load_page(1)
-            nc.sync.dma_start(idx3[:], offs3)
-            load_w3_words(1)
-            raw[0, 1] = load_weight(w1, 1, "w1_raw1", 2)
-            load_page(2)
-            raw[1, 1] = load_weight(w2, 1, "w2_raw1", 3)
-            for i in range(PACK - 1, SLICES):
-                load_page(i)
-            nc.sync.dma_start(out=bias[:], in_=bh.rearrange("(g p t) -> p g t", p=P, t=PACK))
-            nc.sync.dma_start(out=w4_w[:].bitcast(I32), in_=w4_words.rearrange("g p c -> p g c").bitcast(I32))
-            load_scale_rows(nc.sync, w4_s, w4_scales.rearrange("g q n -> q g n"))
-
-        v_w = [keep.tile([P, BANK], U32, name=f"v_w{h}", align_bytes=64) for h in range(2)]
-        v_s = [keep.tile([P, BANK], U8, name=f"v_s{h}", align_bytes=64) for h in range(2)]
-
-        def gather_table(h):
-            part = idx[:, h * 32 : (h + 1) * 32]
-            nc.vector.tensor_copy(v_w[h][:], tab_w[:].indirect(part))
-            nc.vector.tensor_copy(v_s[h][:], tab_s[:].indirect(part))
-
-        codes = [[keep.tile([P, GROUP], I32, name=f"w{n}_codes{g}", align_bytes=64) for g in range(GROUPS)] for n in range(3)]
-        scales = [[keep.tile([P, GROUP], U8, name=f"w{n}_scales{g}", align_bytes=64) for g in range(GROUPS)] for n in range(3)]
-
-        def deal_w3(g):
-            cols = slice(g * GROUP, (g + 1) * GROUP)
-            for dst, src in ((codes[2][g], w3_raw_w[g][:]), (scales[2][g], w3_raw_s[:, cols])):
-                nc.vector.tensor_copy(
-                    out=dst[:].rearrange("p (t m) -> p t m", t=PACK), in_=src.rearrange("p (m t) -> p t m", t=PACK)
-                )
-
-        def woven_tile(name, tag):
-            return slot(name, tag, [P, BANK * PACK], BF16)
-
-        def round_weight(n, g, engine):
-            woven = woven_tile(f"w{n}_woven{g}", f"woven{n}")
-            dst = woven[:].rearrange("p (t m i) -> p m i t", t=PACK, i=PACK)
-            src = raw[n, g][:].rearrange("p i (m t) -> p m i t", t=PACK)
-            if engine == "scalar":
-                nc.scalar.copy(out=dst, in_=src)
-            else:
-                nc.vector.tensor_copy(out=dst, in_=src)
-            return woven
-
-        def quantize_weight(n, g, woven):
-            nc.vector.quantize_mx(out=codes[n][g][:].bitcast(FP8X4), scales=scales[n][g][:], in_=woven[:])
-
-        def product(n, i, h, tag, bufs):
-            g, t = divmod(i, PACK)
-            cols = slice(t * P, (t + 1) * P)
-            acc = psum.tile([P, BANK], F32, name=f"a{n}_{i}_{h}", tag=tag, bufs=bufs)
-            nc.tensor.matmul_mx(
-                out=acc[:], lhsT=codes[n][g][:, cols].bitcast(FP8X4), lhsT_scale=scales[n][g][:, cols],
-                rhs=v_w[h][:].bitcast(FP8X4), rhs_scale=v_s[h][:], start=True, stop=True,
-            )
-            return acc
-
-        damp, value, other = {}, {}, {}
-        on_gpsimd = (2, 3, 4, 5, 6, 7)
-        halves = [slice(h * BANK, (h + 1) * BANK) for h in range(2)]
-
-        def stage_damp(i, parts):
-            damp[i] = slot(f"damp{i}", f"damp{i % 3}", [P, S], F32)
-            for part in parts:
-                for h in range(part.start // BANK, part.stop // BANK):
-                    a3 = product(2, i, h, "a3", 2)
-                    nc.scalar.activation(damp[i][:, halves[h]], a3[:], ACT.Abs)
-                nc.scalar.activation(damp[i][:, part], damp[i][:, part], ACT.Abs_reciprocal_sqrt, bias=1.0)
-                nc.scalar.activation(damp[i][:, part], damp[i][:, part], ACT.Square)
-
-        def stage_value(i):
-            value[i] = slot(f"value{i}", f"value{i % 3}", [P, S], F32)
-            for h in range(2):
-                a2 = product(1, i, h, "a2", 2)
-                nc.scalar.copy(out=value[i][:, halves[h]], in_=a2[:])
-            if i in on_gpsimd:
-                other[i] = slot(f"other{i}", f"other{i % 2}", [P, S], F32)
-                for h in range(2):
-                    a1 = product(0, i, h, "a1", 4)
-                    nc.scalar.copy(out=other[i][:, halves[h]], in_=a1[:])
-
-        def stage_multiply(i):
-            nc.gpsimd.tensor_tensor(damp[i][:], damp[i][:], gains[i % PACK], ALU.mult)
-            if i in on_gpsimd:
-                nc.gpsimd.tensor_tensor(value[i][:], value[i][:], other[i][:], ALU.mult)
-            nc.gpsimd.tensor_tensor(value[i][:], value[i][:], damp[i][:], ALU.mult)
-
-        quads = {}
 
         def store_page(i):
             nc.sync.dma_start(out=page_out[i // PACK, i % PACK], in_=pages[i][:])
 
-        def stage_scatter(i):
-            if i not in on_gpsimd:
-                for h in range(2):
-                    a1 = product(0, i, h, "a1", 4)
-                    nc.vector.tensor_tensor(value[i][:, halves[h]], a1[:], value[i][:, halves[h]], ALU.mult)
+        tab_in = tab_words[0].rearrange("p t i -> p (t i)").bitcast(I32)
+        nc.sync.dma_start(idx[:], offs)
+        nc.sync.dma_start(out=tab_w[:, : T // 2].bitcast(I32), in_=tab_in[:, : T // 2])
+        load_scale_rows(tab_s, tab_scales[0])
+        nc.sync.dma_start(out=w3_raw_w[:], in_=w3_words[0].rearrange("p c i -> p (c i)").bitcast(I32))
+        load_scale_rows(w3_raw_s, w3_scales[0])
+        nc.sync.dma_start(out=tab_w[:, T // 2 :].bitcast(I32), in_=tab_in[:, T // 2 :])
+        load_weight(0, 0)
+        load_weight(1, 0)
+        load_gain(0)
+        nc.sync.dma_start(idx2[:], offs2)
+        load_page(0)
+        load_gain(1)
+        nc.sync.dma_start(idx3[:], offs3)
+        load_weight(0, 1)
+        load_page(1)
+        load_gain(2)
+        load_weight(1, 1)
+        load_gain(3)
+        load_page(2)
+        load_page(3)
+
+        def quantize(codes, scales, woven):
+            nc.vector.quantize_mx(out=codes.bitcast(FP8X4), scales=scales, in_=woven)
+
+        w3_codes = keep.tile([P, H], I32, name="w3_codes", align_bytes=64)
+        w3_dealt_scales = keep.tile([P, H], U8, name="w3_dealt_scales", align_bytes=64)
+        for dst, src in ((w3_dealt_scales, w3_raw_s), (w3_codes, w3_raw_w)):
+            nc.vector.tensor_copy(
+                out=dst[:].rearrange("p (g t m) -> p g t m", g=GROUPS, t=PACK),
+                in_=src[:].rearrange("p (g m t) -> p g t m", g=GROUPS, t=PACK),
+            )
+
+        v_w = [keep.tile([P, BANK], U32, name=f"v_w{h}", align_bytes=64) for h in range(2)]
+        v_s = [keep.tile([P, BANK], U8, name=f"v_s{h}", align_bytes=64) for h in range(2)]
+        for h in range(2):
+            nc.vector.tensor_copy(v_s[h][:], tab_s[:].indirect(entries(idx, halves[h])))
+            nc.vector.tensor_copy(v_w[h][:], tab_w[:].indirect(entries(idx, halves[h])))
+
+        w12_codes = [keep.tile([P, 2 * GROUP], I32, name=f"w12_codes{g}", align_bytes=64) for g in range(GROUPS)]
+        w12_scales = [keep.tile([P, 2 * GROUP], U8, name=f"w12_scales{g}", align_bytes=64) for g in range(GROUPS)]
+
+        def quantize_weights(g, room, copy):
+            woven = lodge(f"w12_woven{g}", room, [P, 2, GROUP * PACK], BF16)
+            for n in range(2):
+                copy(
+                    out=woven[:, n, :].rearrange("p (t m i) -> p m i t", t=PACK, i=PACK),
+                    in_=raw[n, g][:].rearrange("p i (m t) -> p m i t", t=PACK),
+                )
+            quantize(w12_codes[g][:], w12_scales[g][:], woven[:].rearrange("p n c -> p (n c)"))
+
+        def product(n, i, h):
+            g, t = divmod(i, PACK)
+            if n == 2:
+                codes, scales, first = w3_codes, w3_dealt_scales, g * GROUP + t * P
+            else:
+                codes, scales, first = w12_codes[g], w12_scales[g], n * GROUP + t * P
+            acc = bank(f"a{n + 1}_{i}_{h}")
+            nc.tensor.matmul_mx(
+                out=acc[:], lhsT=codes[:, first : first + P].bitcast(FP8X4), lhsT_scale=scales[:, first : first + P],
+                rhs=v_w[h][:].bitcast(FP8X4), rhs_scale=v_s[h][:], start=True, stop=True,
+            )
+            return acc
+
+        damp, value = {}, {}
+
+        def damp_room(i):
+            if i == PACK + 1:
+                return "damp2"
+            return f"damp{(i + (i > PACK + 1)) % 2}"
+
+        def make_damp(i):
+            damp[i] = lodge(f"damp{i}", damp_room(i), [P, S], F32)
+            for h in range(2):
+                nc.scalar.activation(damp[i][:, halves[h]], product(2, i, h)[:], ACT.Abs)
+            for part in halves:
+                nc.scalar.activation(damp[i][:, part], damp[i][:, part], ACT.Abs_reciprocal_sqrt, bias=1.0)
+            for part in halves:
+                nc.scalar.activation(damp[i][:, part], damp[i][:, part], ACT.Square)
+
+        def value_tile(i):
+            return lodge(f"value{i}", f"value{i % AHEAD}", [P, S], F32)
+
+        def make_value(i):
+            value[i] = value_tile(i)
+            other = lodge(f"other{i}", f"other{i % 2}", [P, S], F32)
+            for h in range(2):
+                nc.scalar.copy(out=value[i][:, halves[h]], in_=product(1, i, h)[:])
+                nc.scalar.copy(out=other[:, halves[h]], in_=product(0, i, h)[:])
+            for factor in (gains[i % PACK], other, damp[i]):
+                for part in halves:
+                    nc.gpsimd.tensor_tensor(value[i][:, part], value[i][:, part], factor[:, part], ALU.mult)
+
+        def prepare(i):
+            make_damp(i)
+            make_value(i)
+
+        def scatter(i):
             nc.vector.tensor_copy(pages[i][:].indirect(idx2[:]), value[i][:])
 
-        def first_slice():
-            stage_damp(0, halves)
-            value[0] = slot("value0", "value0", [P, S], F32)
-            for h in range(2):
-                nc.gpsimd.tensor_tensor(damp[0][:, halves[h]], damp[0][:, halves[h]], gains[0][:, halves[h]], ALU.mult)
-            for h in range(2):
-                a2 = product(1, 0, h, "a2", 2)
-                nc.vector.tensor_tensor(value[0][:, halves[h]], a2[:], damp[0][:, halves[h]], ALU.mult)
+        quads = {}
 
         def regroup(i):
             g, t = divmod(i, PACK)
@@ -218,133 +212,148 @@ def tile_list_digester_feed_features_kernel(
             for c in range(CHUNKS):
                 nc.sync.dma_start(out=quads[g][c][:, t, :], in_=pages[i][:, c * BANK : (c + 1) * BANK])
 
-        page_woven, page_scales = {}, {}
+        def weave(woven, rows, count):
+            nc.scalar.copy(
+                out=woven.rearrange("p (c i t) -> p c t i", i=RUN, t=PACK)[:, :, :count, :],
+                in_=rows[:, :count, :].rearrange("p t (c i) -> p c t i", i=RUN),
+            )
 
-        def weave(engine, dst, src):
-            dst = dst.rearrange("p (c i t) -> p c t i", i=4, t=PACK)
-            src = src.rearrange("p t (c i) -> p c t i", i=4)
-            if engine == "scalar":
-                nc.scalar.copy(out=dst, in_=src)
-            elif engine == "vector":
-                nc.vector.tensor_copy(out=dst, in_=src)
-            else:
-                nc.gpsimd.tensor_scalar(dst, src, 1.0, 0.0, ALU.mult, ALU.add)
+        def last_row(woven):
+            return woven.rearrange("p (c t) -> p t c", t=PACK)[:, PACK - 1, :]
 
-        def round_page(g, c, tag, engine):
-            page_woven[g, c] = woven_tile(f"page_woven{g}_{c}", tag)
-            weave(engine, page_woven[g, c][:], quads[g][c][:])
+        page_scales = [keep.tile([P, T2], U8, name=f"page_scales{g}", align_bytes=64) for g in range(GROUPS)]
 
-        def quantize_page(g, c):
-            if c == 0:
-                page_scales[g] = work.tile([P, T2], U8, name=f"page_scales{g}", tag="page_scales", bufs=2, align_bytes=64)
-            cols = slice(c * BANK, (c + 1) * BANK)
-            words = work.tile([P, BANK], I32, name=f"page_words{g}_{c}", tag="page_words", bufs=3, align_bytes=64)
-            nc.vector.quantize_mx(out=words[:].bitcast(FP8X4), scales=page_scales[g][:, cols], in_=page_woven[g, c][:])
+        def quantize_page(g, cols, woven, room):
+            words = lodge(f"page_words{g}_{cols.start}", room, [P, cols.stop - cols.start], I32)
+            quantize(words[:], page_scales[g][:, cols], woven)
+            return words
+
+        def store_words(g, cols, words):
             nc.sync.dma_start(out=out_2[g].rearrange("p m t -> p (m t)").bitcast(I32)[:, cols], in_=words[:])
-            if c == CHUNKS - 1:
-                for q in range(4):
-                    nc.sync.dma_start(
-                        out=out_3[g, 4 * q : 4 * q + 4].bitcast(I32), in_=page_scales[g][32 * q : 32 * q + 4].bitcast(I32)
-                    )
 
-        x_rows, x_woven = {}, {}
-        x_codes = [[keep.tile([P, BANK], I32, name=f"x_codes{g}_{h}", align_bytes=64) for h in range(2)] for g in range(GROUPS)]
-        x_scales = [[keep.tile([P, BANK], U8, name=f"x_scales{g}_{h}", align_bytes=64) for h in range(2)] for g in range(GROUPS)]
+        def store_page_scales(g):
+            for q in QUADRANT_ORDER:
+                rows = page_scales[g][QUADRANT * q : QUADRANT * q + 4]
+                nc.sync.dma_start(out=out_3[g, 4 * q : 4 * q + 4].bitcast(I32), in_=rows.bitcast(I32))
 
-        picked = [keep.tile([P, NP], F32, name=f"picked{t}") for t in range(PACK)]
+        x_codes = [keep.tile([P, NP], I32, name=f"x_codes{g}", align_bytes=64) for g in range(GROUPS)]
+        x_scales = [keep.tile([P, NP], U8, name=f"x_scales{g}", align_bytes=64) for g in range(GROUPS)]
 
-        def gather_page(i, cols):
-            part = idx3[:, cols.start // 16 : cols.stop // 16]
-            nc.vector.tensor_copy(picked[i % PACK][:, cols], pages[i][:].indirect(part))
-
-        def add_bias(i, cols):
-            g, t = divmod(i, PACK)
-            if g not in x_rows:
-                x_rows[g] = slot(f"x_rows{g}", f"damp{2 - g}", [P, PACK, NP], BF16)
-            nc.gpsimd.tensor_scalar(x_rows[g][:, t, cols], picked[t][:, cols], 1.0, bias[:, g, t : t + 1], ALU.mult, ALU.add)
-
-        def weave_x(g, h, tag, engine):
-            x_woven[g, h] = woven_tile(f"x_woven{g}_{h}", tag)
-            weave(engine, x_woven[g, h][:], x_rows[g][:, :, halves[h]])
-
-        def quantize_x(g, h):
-            nc.vector.quantize_mx(out=x_codes[g][h][:].bitcast(FP8X4), scales=x_scales[g][h][:], in_=x_woven[g, h][:])
-
-        def features(h):
+        def features(h, room):
+            staged = lodge(f"y_staged{h}", room, [P, N // P, BANK], F32)
             for n in range(N // P):
-                tag, bufs = (("a1", 4), ("a2", 2), ("a3", 2))[n]
-                acc = psum.tile([P, BANK], F32, name=f"y{n}_{h}", tag=tag, bufs=bufs)
+                acc = bank(f"y{n}_{h}")
                 for g in range(GROUPS):
                     nc.tensor.matmul_mx(
                         out=acc[:], lhsT=w4_w[:, g, 2 * n * P : 2 * (n + 1) * P].bitcast(FP4X4),
                         lhsT_scale=w4_s[:, g, n * P : (n + 1) * P],
-                        rhs=x_codes[g][h][:].bitcast(FP8X4), rhs_scale=x_scales[g][h][:],
+                        rhs=x_codes[g][:, halves[h]].bitcast(FP8X4), rhs_scale=x_scales[g][:, halves[h]],
                         start=(g == 0), stop=(g == GROUPS - 1),
                     )
-                staged = slot(f"y_staged{n}_{h}", (f"value{n}" if h == 0 else ("other0", "other1", "damp0")[n]), [P, BANK], F32)
-                if True:
-                    nc.scalar.copy(out=staged[:], in_=acc[:])
-                else:
-                    nc.vector.tensor_copy(out=staged[:], in_=acc[:])
-                nc.sync.dma_start(out=out_0[n * P : (n + 1) * P, h * BANK : (h + 1) * BANK], in_=staged[:])
+                nc.vector.tensor_copy(out=staged[:, n, :], in_=acc[:])
+                nc.sync.dma_start(out=out_0[n * P : (n + 1) * P, halves[h]], in_=staged[:, n, :])
 
-        whole = [slice(0, S)]
-        gather_table(0)
-        deal_w3(0)
-        woven1 = round_weight(0, 0, "scalar")
-        gather_table(1)
-        load_rest()
-        woven2 = round_weight(1, 0, "vector")
-        quantize_weight(1, 0, woven2)
-        quantize_weight(0, 0, woven1)
-        first_slice()
-        for i in range(1, 3):
-            stage_damp(i, whole)
-            stage_value(i)
-            stage_multiply(i)
-        last = SLICES - 1
-        for i in range(last):
-            stage_scatter(i)
+        quantize_weights(0, "woven0", nc.vector.tensor_copy)
+        make_damp(0)
+        make_damp(1)
+        value[0] = value_tile(0)
+        nc.vector.tensor_tensor(damp[0][:], damp[0][:], gains[0][:], ALU.mult)
+        for h in range(2):
+            nc.vector.tensor_tensor(value[0][:, halves[h]], product(0, 0, h)[:], damp[0][:, halves[h]], ALU.mult)
+            nc.vector.tensor_tensor(value[0][:, halves[h]], product(1, 0, h)[:], value[0][:, halves[h]], ALU.mult)
+        make_value(1)
+        prepare(2)
+
+        picked = lodge("picked", "table", [P, PACK, NP], F32)
+
+        def gather_page(i, cols):
+            nc.vector.tensor_copy(picked[:, i % PACK, cols], pages[i][:].indirect(entries(idx3, cols)))
+
+        pairs = [slice(0, T2 // 2), slice(T2 // 2, T2)]
+        pair_woven = []
+
+        def weave_pair(k):
+            pair_woven.append(lodge(f"page_woven0_{k}", f"woven{k}", [P, 2, BANK * PACK], BF16))
+            for j in range(2):
+                weave(pair_woven[k][:, j, :], quads[0][2 * k + j][:], PACK)
+
+        for i in range(PACK):
+            scatter(i)
             if i == 0:
-                deal_w3(1)
-                woven1 = round_weight(0, 1, "scalar")
-                woven2 = round_weight(1, 1, "scalar")
-                quantize_weight(0, 1, woven1)
-                quantize_weight(1, 1, woven2)
-            if i + 3 < SLICES:
-                stage_damp(i + 3, whole)
-                stage_value(i + 3)
-                stage_multiply(i + 3)
-            if i == PACK:
-                for k in range(PACK):
-                    add_bias(k, whole[0])
-                for c in range(CHUNKS):
-                    round_page(0, c, f"woven{c % 3}", "scalar")
-                    quantize_page(0, c)
-                for h in range(2):
-                    weave_x(0, h, f"woven{1 + h}", "scalar")
-                    quantize_x(0, h)
-            gather_page(i, whole[0])
-            if i >= PACK:
-                add_bias(i, whole[0])
+                quantize_weights(1, "damp2", nc.scalar.copy)
             regroup(i)
+            if i == PACK - 2:
+                load_page(PACK)
+            if i == PACK - 1:
+                load_page(PACK + 1)
+                load_page(PACK + 2)
+                nc.sync.dma_start(out=bias[:], in_=bh.rearrange("(g p t) -> p g t", p=P, t=PACK))
+                nc.sync.dma_start(out=w4_w[:].bitcast(I32), in_=w4_words.rearrange("g p c -> p g c").bitcast(I32))
+                load_scale_rows(w4_s, w4_scales.rearrange("g q n -> q g n"))
+                weave_pair(0)
+            prepare(i + AHEAD)
+            gather_page(i, whole)
+        for i in range(PACK):
             store_page(i)
-        stage_scatter(last)
-        regroup(last)
-        store_page(last)
+
+        scatter(PACK)
+        weave_pair(1)
+        pair_words = [quantize_page(0, pairs[0], pair_woven[0][:].rearrange("p j c -> p (j c)"), "words0")]
+        prepare(LAST)
+        x_rows = lodge("x_rows0", "damp2", [P, PACK, NP], BF16)
+        for t in range(PACK):
+            nc.scalar.activation(x_rows[:, t, :], picked[:, t, :], ACT.Identity, bias=bias[:, 0, t : t + 1])
+        x_woven = lodge("x_woven0", "woven0", [P, NP * PACK], BF16)
+        weave(x_woven[:], x_rows[:], PACK)
+        pair_words.append(quantize_page(0, pairs[1], pair_woven[1][:].rearrange("p j c -> p (j c)"), "damp1"))
+        quantize(x_codes[0][:], x_scales[0][:], x_woven[:])
+
+        early_rows = lodge("x_rows1", "damp0", [P, PACK - 1, NP], BF16)
+        for i in range(PACK, LAST):
+            t = i % PACK
+            if i > PACK:
+                scatter(i)
+            gather_page(i, whole)
+            nc.gpsimd.tensor_scalar(early_rows[:, t, :], picked[:, t, :], 1.0, bias[:, 1, t : t + 1], ALU.mult, ALU.add)
+            regroup(i)
+        load_page(LAST)
+        for k in range(2):
+            store_page(PACK + k)
+            store_words(0, pairs[k], pair_words[k])
+        store_page_scales(0)
+        store_page(LAST - 1)
+
+        chunks = [slice(c * BANK, (c + 1) * BANK) for c in range(CHUNKS)]
+        chunk_woven = []
+        for c, room in enumerate(("other0", "other1", "value2", "woven2")):
+            chunk_woven.append(lodge(f"page_woven1_{c}", room, [P, BANK * PACK], BF16))
+            weave(chunk_woven[c][:], quads[1][c][:], PACK - 1)
+        half_woven = []
         for h in range(2):
-            gather_page(last, halves[h])
-            add_bias(last, halves[h])
-            weave_x(1, h, f"woven{h}", "scalar")
-        round_page(1, 3, "value2", "gpsimd")
-        round_page(1, 0, "woven2", "vector")
-        round_page(1, 1, "value0", "vector")
-        quantize_x(1, 0)
-        quantize_page(1, 0)
-        quantize_page(1, 1)
-        quantize_x(1, 1)
-        round_page(1, 2, "value1", "vector")
-        quantize_page(1, 2)
-        quantize_page(1, 3)
+            half_woven.append(lodge(f"x_woven1_{h}", f"quad{h + 1}", [P, BANK * PACK], BF16))
+            weave(half_woven[h][:], early_rows[:, :, halves[h]], PACK - 1)
+
+        def finish_chunk(c):
+            nc.scalar.copy(out=last_row(chunk_woven[c][:]), in_=pages[LAST][:, chunks[c]])
+
+        def emit_chunk(c, room):
+            store_words(1, chunks[c], quantize_page(1, chunks[c], chunk_woven[c][:], room))
+
+        scatter(LAST)
+        store_page(LAST)
+        finish_chunk(0)
         for h in range(2):
-            features(h)
+            gather_page(LAST, halves[h])
+            nc.scalar.activation(
+                last_row(half_woven[h][:]), picked[:, PACK - 1, halves[h]], ACT.Identity, bias=bias[:, 1, PACK - 1 : PACK]
+            )
+        for c in range(1, CHUNKS):
+            finish_chunk(c)
+        emit_chunk(0, "words0")
+        for h in range(2):
+            quantize(x_codes[1][:, halves[h]], x_scales[1][:, halves[h]], half_woven[h][:])
+        features(0, "woven0")
+        features(1, "quad0")
+        for c, room in ((1, "woven1"), (2, "damp2"), (3, "value1")):
+            emit_chunk(c, room)
+        store_page_scales(1)

@@ -68,9 +68,11 @@ def tile_list_digester_feed_features_kernel(
         bias = keep.tile([P, GROUPS, PACK], F32, name="bias")
         gains = [keep.tile([P, S], F32, name=f"gain{t}") for t in range(PACK)]
         pages = [keep.tile([P, T2], F32, name=f"page{i}") for i in range(SLICES)]
+        warm = keep.tile([P, 2], F32, name="warm")
 
         nc.vector.memset(tab_s[:].bitcast(I32), 0)
         nc.vector.memset(w3_raw_s[:].bitcast(I32), 0)
+        nc.vector.memset(warm[:], 1.0)
         nc.vector.memset(w4_s[:].rearrange("p g n -> p (g n)").bitcast(I32), 0)
 
         def load_scale_rows(plane, rows):
@@ -111,6 +113,7 @@ def tile_list_digester_feed_features_kernel(
         load_scale_rows(w3_raw_s, w3_scales[0])
         nc.sync.dma_start(out=tab_w[:, T // 2 :].bitcast(I32), in_=tab_in[:, T // 2 :])
         load_weight(0, 0)
+        nc.scalar.activation(warm[:, 1:2], warm[:, 0:1], ACT.Abs_reciprocal_sqrt)
         load_weight(1, 0)
         load_gain(0)
         nc.sync.dma_start(idx2[:], offs2)

from contextlib import ExitStack

import concourse.mybir as mybir

K, T, S, H, T2, NP, N = 512, 4096, 1024, 1024, 2048, 1024, 384
FLOPS = 2 * K * H * S * 3 + 2 * H * N * NP

F32 = mybir.dt.float32
BF16 = mybir.dt.bfloat16
I32 = mybir.dt.int32
U32 = mybir.dt.uint32
U16 = mybir.dt.uint16
U8 = mybir.dt.uint8
FP8X4 = mybir.dt.float8_e4m3fn_x4
FP4X4 = mybir.dt.float4_e2m1fn_x4
ACT = mybir.ActivationFunctionType
ALU = mybir.AluOpType

P = 128
PACK = 4
GROUP = P * PACK
BANK = 512
PSUM_BANKS = 8
QUADRANT = 32
QUADRANT_ORDER = (0, 2, 1, 3)
LIST_ROWS = 16
RUN = 4
GROUPS = H // GROUP
SLICES = GROUPS * PACK
LAST = SLICES - 1
CHUNKS = T2 // BANK
AHEAD = 3


def tile_list_digester_feed_features_kernel(
    tc, tab_words, tab_scales, offs, offs2, offs3, w1, w2, w3_words, w3_scales, page0, wgs, bh, w4_words, w4_scales,
    out_0, out_1, out_2, out_3,
):
    nc = tc.nc
    with ExitStack() as ctx:
        lists = ctx.enter_context(tc.tile_pool(name="lists", bufs=1))
        keep = ctx.enter_context(tc.tile_pool(name="keep", bufs=1))
        work = ctx.enter_context(tc.tile_pool(name="work", bufs=1))
        psum = ctx.enter_context(tc.psum_pool(name="psum", bufs=1))

        def lodge(name, room, shape, dtype):
            return work.tile(shape, dtype, name=name, tag=room, align_bytes=64)

        def bank(name):
            return psum.tile([P, BANK], F32, name=name, tag="bank", bufs=PSUM_BANKS)

        halves = [slice(h * BANK, (h + 1) * BANK) for h in range(2)]
        whole = slice(0, NP)

        idx = lists.tile([P, S // LIST_ROWS], U16, name="idx")
        idx2 = lists.tile([P, S // LIST_ROWS], U16, name="idx2")
        idx3 = lists.tile([P, NP // LIST_ROWS], U16, name="idx3")

        def entries(offsets, cols):
            return offsets[:, cols.start // LIST_ROWS : cols.stop // LIST_ROWS]

        tab_w = lodge("tab_w", "table", [P, T], U32)
        tab_s = lodge("tab_s", "woven2", [P, T], U8)
        w3_raw_w = keep.tile([P, H], I32, name="w3_raw_w", align_bytes=64)
        w3_raw_s = keep.tile([P, H], U8, name="w3_raw_s", align_bytes=64)
        w4_w = keep.tile([P, GROUPS, 2 * N], U8, name="w4_w", align_bytes=64)
        w4_s = keep.tile([P, GROUPS, N], U8, name="w4_s", align_bytes=64)
        bias = keep.tile([P, GROUPS, PACK], F32, name="bias")
        gains = [keep.tile([P, S], F32, name=f"gain{t}") for t in range(PACK)]
        pages = [keep.tile([P, T2], F32, name=f"page{i}") for i in range(SLICES)]
        warm = keep.tile([P, 2], F32, name="warm")

        nc.vector.memset(tab_s[:].bitcast(I32), 0)
        nc.vector.memset(w3_raw_s[:].bitcast(I32), 0)
        nc.vector.memset(warm[:], 1.0)
        nc.vector.memset(w4_s[:].rearrange("p g n -> p (g n)").bitcast(I32), 0)

        def load_scale_rows(plane, rows):
            for q in QUADRANT_ORDER:
                nc.sync.dma_start(
                    out=plane[QUADRANT * q : QUADRANT * q + 4].bitcast(I32), in_=rows[4 * q : 4 * q + 4].bitcast(I32)
                )

        def quad_tile(name, c):
            return lodge(name, f"quad{c}", [P, PACK, BANK], F32)

        raw = {}

        def load_weight(n, g):
            raw[n, g] = quad_tile(f"w{n + 1}_raw{g}", 2 * g + n)
            cols = (w1, w2)[n][:, g * GROUP : (g + 1) * GROUP]
            nc.sync.dma_start(out=raw[n, g][:], in_=cols.rearrange("(p i) c -> p i c", i=PACK))

        def load_gain(t):
            rows = wgs.rearrange("(q t) j -> t q j", t=PACK)[t]
            for q in QUADRANT_ORDER:
                nc.sync.dma_start(out=gains[t][QUADRANT * q : QUADRANT * (q + 1)], in_=rows)

        page_in = page0.rearrange("(g p t) m -> g t p m", p=P, t=PACK)
        page_out = out_1.rearrange("(g p t) m -> g t p m", p=P, t=PACK)

        def load_page(i):
            nc.sync.dma_start(out=pages[i][:], in_=page_in[i // PACK, i % PACK])

        def store_page(i):
            nc.sync.dma_start(out=page_out[i // PACK, i % PACK], in_=pages[i][:])

        tab_in = tab_words[0].rearrange("p t i -> p (t i)").bitcast(I32)
        nc.sync.dma_start(idx[:], offs)
        nc.sync.dma_start(out=tab_w[:, : T // 2].bitcast(I32), in_=tab_in[:, : T // 2])
        load_scale_rows(tab_s, tab_scales[0])
        nc.sync.dma_start(out=w3_raw_w[:], in_=w3_words[0].rearrange("p c i -> p (c i)").bitcast(I32))
        load_scale_rows(w3_raw_s, w3_scales[0])
        nc.sync.dma_start(out=tab_w[:, T // 2 :].bitcast(I32), in_=tab_in[:, T // 2 :])
        load_weight(0, 0)
        nc.scalar.activation(warm[:, 1:2], warm[:, 0:1], ACT.Abs_reciprocal_sqrt)
        load_weight(1, 0)
        load_gain(0)
        nc.sync.dma_start(idx2[:], offs2)
        load_page(0)
        load_gain(1)
        nc.sync.dma_start(idx3[:], offs3)
        load_weight(0, 1)
        load_page(1)
        load_gain(2)
        load_weight(1, 1)
        load_gain(3)
        load_page(2)
        load_page(3)

        def quantize(codes, scales, woven):
            nc.vector.quantize_mx(out=codes.bitcast(FP8X4), scales=scales, in_=woven)

        w3_codes = keep.tile([P, H], I32, name="w3_codes", align_bytes=64)
        w3_dealt_scales = keep.tile([P, H], U8, name="w3_dealt_scales", align_bytes=64)
        for dst, src in ((w3_dealt_scales, w3_raw_s), (w3_codes, w3_raw_w)):
            nc.vector.tensor_copy(
                out=dst[:].rearrange("p (g t m) -> p g t m", g=GROUPS, t=PACK),
                in_=src[:].rearrange("p (g m t) -> p g t m", g=GROUPS, t=PACK),
            )

        v_w = [keep.tile([P, BANK], U32, name=f"v_w{h}", align_bytes=64) for h in range(2)]
        v_s = [keep.tile([P, BANK], U8, name=f"v_s{h}", align_bytes=64) for h in range(2)]
        for h in range(2):
            nc.vector.tensor_copy(v_s[h][:], tab_s[:].indirect(entries(idx, halves[h])))
            nc.vector.tensor_copy(v_w[h][:], tab_w[:].indirect(entries(idx, halves[h])))

        w12_codes = [keep.tile([P, 2 * GROUP], I32, name=f"w12_codes{g}", align_bytes=64) for g in range(GROUPS)]
        w12_scales = [keep.tile([P, 2 * GROUP], U8, name=f"w12_scales{g}", align_bytes=64) for g in range(GROUPS)]

        def quantize_weights(g, room, copy):
            woven = lodge(f"w12_woven{g}", room, [P, 2, GROUP * PACK], BF16)
            for n in range(2):
                copy(
                    out=woven[:, n, :].rearrange("p (t m i) -> p m i t", t=PACK, i=PACK),
                    in_=raw[n, g][:].rearrange("p i (m t) -> p m i t", t=PACK),
                )
            quantize(w12_codes[g][:], w12_scales[g][:], woven[:].rearrange("p n c -> p (n c)"))

        def product(n, i, h):
            g, t = divmod(i, PACK)
            if n == 2:
                codes, scales, first = w3_codes, w3_dealt_scales, g * GROUP + t * P
            else:
                codes, scales, first = w12_codes[g], w12_scales[g], n * GROUP + t * P
            acc = bank(f"a{n + 1}_{i}_{h}")
            nc.tensor.matmul_mx(
                out=acc[:], lhsT=codes[:, first : first + P].bitcast(FP8X4), lhsT_scale=scales[:, first : first + P],
                rhs=v_w[h][:].bitcast(FP8X4), rhs_scale=v_s[h][:], start=True, stop=True,
            )
            return acc

        damp, value = {}, {}

        def damp_room(i):
            if i == PACK + 1:
                return "damp2"
            return f"damp{(i + (i > PACK + 1)) % 2}"

        def make_damp(i):
            damp[i] = lodge(f"damp{i}", damp_room(i), [P, S], F32)
            for h in range(2):
                nc.scalar.activation(damp[i][:, halves[h]], product(2, i, h)[:], ACT.Abs)
            for part in halves:
                nc.scalar.activation(damp[i][:, part], damp[i][:, part], ACT.Abs_reciprocal_sqrt, bias=1.0)
            for part in halves:
                nc.scalar.activation(damp[i][:, part], damp[i][:, part], ACT.Square)

        def value_tile(i):
            return lodge(f"value{i}", f"value{i % AHEAD}", [P, S], F32)

        def make_value(i):
            value[i] = value_tile(i)
            other = lodge(f"other{i}", f"other{i % 2}", [P, S], F32)
            for h in range(2):
                nc.scalar.copy(out=value[i][:, halves[h]], in_=product(1, i, h)[:])
                nc.scalar.copy(out=other[:, halves[h]], in_=product(0, i, h)[:])
            for factor in (gains[i % PACK], other, damp[i]):
                for part in halves:
                    nc.gpsimd.tensor_tensor(value[i][:, part], value[i][:, part], factor[:, part], ALU.mult)

        def prepare(i):
            make_damp(i)
            make_value(i)

        def scatter(i):
            nc.vector.tensor_copy(pages[i][:].indirect(idx2[:]), value[i][:])

        quads = {}

        def regroup(i):
            g, t = divmod(i, PACK)
            if t == 0:
                quads[g] = [quad_tile(f"quad{g}_{c}", c) for c in range(CHUNKS)]
            for c in range(CHUNKS):
                nc.sync.dma_start(out=quads[g][c][:, t, :], in_=pages[i][:, c * BANK : (c + 1) * BANK])

        def weave(woven, rows, count):
            nc.scalar.copy(
                out=woven.rearrange("p (c i t) -> p c t i", i=RUN, t=PACK)[:, :, :count, :],
                in_=rows[:, :count, :].rearrange("p t (c i) -> p c t i", i=RUN),
            )

        def last_row(woven):
            return woven.rearrange("p (c t) -> p t c", t=PACK)[:, PACK - 1, :]

        page_scales = [keep.tile([P, T2], U8, name=f"page_scales{g}", align_bytes=64) for g in range(GROUPS)]

        def quantize_page(g, cols, woven, room):
            words = lodge(f"page_words{g}_{cols.start}", room, [P, cols.stop - cols.start], I32)
            quantize(words[:], page_scales[g][:, cols], woven)
            return words

        def store_words(g, cols, words):
            nc.sync.dma_start(out=out_2[g].rearrange("p m t -> p (m t)").bitcast(I32)[:, cols], in_=words[:])

        def store_page_scales(g):
            for q in QUADRANT_ORDER:
                rows = page_scales[g][QUADRANT * q : QUADRANT * q + 4]
                nc.sync.dma_start(out=out_3[g, 4 * q : 4 * q + 4].bitcast(I32), in_=rows.bitcast(I32))

        x_codes = [keep.tile([P, NP], I32, name=f"x_codes{g}", align_bytes=64) for g in range(GROUPS)]
        x_scales = [keep.tile([P, NP], U8, name=f"x_scales{g}", align_bytes=64) for g in range(GROUPS)]

        def features(h, room):
            staged = lodge(f"y_staged{h}", room, [P, N // P, BANK], F32)
            for n in range(N // P):
                acc = bank(f"y{n}_{h}")
                for g in range(GROUPS):
                    nc.tensor.matmul_mx(
                        out=acc[:], lhsT=w4_w[:, g, 2 * n * P : 2 * (n + 1) * P].bitcast(FP4X4),
                        lhsT_scale=w4_s[:, g, n * P : (n + 1) * P],
                        rhs=x_codes[g][:, halves[h]].bitcast(FP8X4), rhs_scale=x_scales[g][:, halves[h]],
                        start=(g == 0), stop=(g == GROUPS - 1),
                    )
                nc.vector.tensor_copy(out=staged[:, n, :], in_=acc[:])
                nc.sync.dma_start(out=out_0[n * P : (n + 1) * P, halves[h]], in_=staged[:, n, :])

        quantize_weights(0, "woven0", nc.vector.tensor_copy)
        make_damp(0)
        make_damp(1)
        value[0] = value_tile(0)
        nc.vector.tensor_tensor(damp[0][:], damp[0][:], gains[0][:], ALU.mult)
        for h in range(2):
            nc.vector.tensor_tensor(value[0][:, halves[h]], product(0, 0, h)[:], damp[0][:, halves[h]], ALU.mult)
            nc.vector.tensor_tensor(value[0][:, halves[h]], product(1, 0, h)[:], value[0][:, halves[h]], ALU.mult)
        make_value(1)
        prepare(2)

        picked = lodge("picked", "table", [P, PACK, NP], F32)

        def gather_page(i, cols):
            nc.vector.tensor_copy(picked[:, i % PACK, cols], pages[i][:].indirect(entries(idx3, cols)))

        pairs = [slice(0, T2 // 2), slice(T2 // 2, T2)]
        pair_woven = []

        def weave_pair(k):
            pair_woven.append(lodge(f"page_woven0_{k}", f"woven{k}", [P, 2, BANK * PACK], BF16))
            for j in range(2):
                weave(pair_woven[k][:, j, :], quads[0][2 * k + j][:], PACK)

        for i in range(PACK):
            scatter(i)
            if i == 0:
                quantize_weights(1, "damp2", nc.scalar.copy)
            regroup(i)
            if i == PACK - 2:
                load_page(PACK)
            if i == PACK - 1:
                load_page(PACK + 1)
                load_page(PACK + 2)
                nc.sync.dma_start(out=bias[:], in_=bh.rearrange("(g p t) -> p g t", p=P, t=PACK))
                nc.sync.dma_start(out=w4_w[:].bitcast(I32), in_=w4_words.rearrange("g p c -> p g c").bitcast(I32))
                load_scale_rows(w4_s, w4_scales.rearrange("g q n -> q g n"))
                weave_pair(0)
            prepare(i + AHEAD)
            gather_page(i, whole)
        for i in range(PACK):
            store_page(i)

        scatter(PACK)
        weave_pair(1)
        pair_words = [quantize_page(0, pairs[0], pair_woven[0][:].rearrange("p j c -> p (j c)"), "words0")]
        prepare(LAST)
        x_rows = lodge("x_rows0", "damp2", [P, PACK, NP], BF16)
        for t in range(PACK):
            nc.scalar.activation(x_rows[:, t, :], picked[:, t, :], ACT.Identity, bias=bias[:, 0, t : t + 1])
        x_woven = lodge("x_woven0", "woven0", [P, NP * PACK], BF16)
        weave(x_woven[:], x_rows[:], PACK)
        pair_words.append(quantize_page(0, pairs[1], pair_woven[1][:].rearrange("p j c -> p (j c)"), "damp1"))
        quantize(x_codes[0][:], x_scales[0][:], x_woven[:])

        early_rows = lodge("x_rows1", "damp0", [P, PACK - 1, NP], BF16)
        for i in range(PACK, LAST):
            t = i % PACK
            if i > PACK:
                scatter(i)
            gather_page(i, whole)
            nc.gpsimd.tensor_scalar(early_rows[:, t, :], picked[:, t, :], 1.0, bias[:, 1, t : t + 1], ALU.mult, ALU.add)
            regroup(i)
        load_page(LAST)
        for k in range(2):
            store_page(PACK + k)
            store_words(0, pairs[k], pair_words[k])
        store_page_scales(0)
        store_page(LAST - 1)

        chunks = [slice(c * BANK, (c + 1) * BANK) for c in range(CHUNKS)]
        chunk_woven = []
        for c, room in enumerate(("other0", "other1", "value2", "woven2")):
            chunk_woven.append(lodge(f"page_woven1_{c}", room, [P, BANK * PACK], BF16))
            weave(chunk_woven[c][:], quads[1][c][:], PACK - 1)
        half_woven = []
        for h in range(2):
            half_woven.append(lodge(f"x_woven1_{h}", f"quad{h + 1}", [P, BANK * PACK], BF16))
            weave(half_woven[h][:], early_rows[:, :, halves[h]], PACK - 1)

        def finish_chunk(c):
            nc.scalar.copy(out=last_row(chunk_woven[c][:]), in_=pages[LAST][:, chunks[c]])

        def emit_chunk(c, room):
            store_words(1, chunks[c], quantize_page(1, chunks[c], chunk_woven[c][:], room))

        scatter(LAST)
        store_page(LAST)
        finish_chunk(0)
        for h in range(2):
            gather_page(LAST, halves[h])
            nc.scalar.activation(
                last_row(half_woven[h][:]), picked[:, PACK - 1, halves[h]], ACT.Identity, bias=bias[:, 1, PACK - 1 : PACK]
            )
        for c in range(1, CHUNKS):
            finish_chunk(c)
        emit_chunk(0, "words0")
        for h in range(2):
            quantize(x_codes[1][:, halves[h]], x_scales[1][:, halves[h]], half_woven[h][:])
        features(0, "woven0")
        features(1, "quad0")
        for c, room in ((1, "woven1"), (2, "damp2"), (3, "value1")):
            emit_chunk(c, room)
        store_page_scales(1)
